import numpy as np
import ml_dtypes

BF16 = ml_dtypes.bfloat16


def bf(x):
    return np.asarray(x, np.float32).astype(BF16)


def f32(x):
    return np.asarray(x, np.float32)


def f64(x):
    return np.asarray(x).astype(np.float64)


def striped(idx):
    return np.tile(idx.reshape(-1, 16).T, (8, 1))


S, K, M, N = 256, 512, 128, 64


def setup_inputs():
    return {"base": bf(np.random.standard_normal((M, S))), "x": bf(np.random.standard_normal((K, N))), "w": bf(np.random.standard_normal((K, M)) / np.sqrt(K)), "offs": striped(np.random.permutation(S)[:N])}


def reference(base, x, w, offs):
    idx = offs[:16].T.reshape(-1)
    z = f64(base).copy()
    z[:, idx] += f64(w).T @ f64(x)
    return z

@@ -1,0 +1,49 @@
+import concourse.mybir as mybir
+from concourse.masks import make_identity
+
+BF16, F32, U16 = mybir.dt.bfloat16, mybir.dt.float32, mybir.dt.uint16
+
+P = 128
+S = 256
+N = 64
+K = 512
+BLOCKS = K // P
+
+FLOPS = 2 * K * P * N
+
+
+def tile_scatter_matmul_kernel(tc, base, x, w, offs, out):
+    nc = tc.nc
+    with (
+        tc.tile_pool(name="held", bufs=1) as held,
+        tc.psum_pool(name="psum", bufs=1) as psum,
+    ):
+        offsets = held.tile([P, N // 16], U16, name="offsets")
+        nc.sync.dma_start(offsets[:], offs)
+
+        base_tile = held.tile([P, S], BF16, name="base_tile")
+        nc.scalar.dma_start(base_tile[:], base)
+
+        w_tile = held.tile([P, BLOCKS * P], BF16, name="w_tile")
+        nc.sync.dma_start(w_tile[:], w.rearrange("(p a) m -> p (a m)", a=BLOCKS))
+        x_tile = held.tile([P, BLOCKS * N], BF16, name="x_tile")
+        nc.scalar.dma_start(x_tile[:], x.rearrange("(p a) j -> p (a j)", a=BLOCKS))
+
+        identity = held.tile([P, P], BF16, name="identity")
+        make_identity(nc, identity[:])
+
+        window = psum.tile([P, S], F32, name="window")
+        nc.tensor.matmul(window[:], identity[:], base_tile[:], start=True, stop=False)
+
+        for a in range(BLOCKS):
+            nc.tensor.matmul(
+                window[:].indirect(offsets[:]),
+                w_tile[:, a * P : (a + 1) * P],
+                x_tile[:, a * N : (a + 1) * N],
+                start=False,
+                stop=(a == BLOCKS - 1),
+            )
+
+        z = held.tile([P, S], F32, name="z")
+        nc.vector.tensor_copy(z[:], window[:])
+        nc.sync.dma_start(out, z[:])

@@ -18,16 +18,18 @@ def tile_scatter_matmul_kernel(tc, base, x, w, offs, out):
         tc.tile_pool(name="held", bufs=1) as held,
         tc.psum_pool(name="psum", bufs=1) as psum,
     ):
-        offsets = held.tile([P, N // 16], U16, name="offsets")
-        nc.sync.dma_start(offsets[:], offs)
+        w_rows = w.rearrange("(p a) m -> p (a m)", a=BLOCKS)
+        x_rows = x.rearrange("(p a) j -> p (a j)", a=BLOCKS)
 
         base_tile = held.tile([P, S], BF16, name="base_tile")
-        nc.scalar.dma_start(base_tile[:], base)
-
-        w_tile = held.tile([P, BLOCKS * P], BF16, name="w_tile")
-        nc.sync.dma_start(w_tile[:], w.rearrange("(p a) m -> p (a m)", a=BLOCKS))
+        offsets = held.tile([P, N // 16], U16, name="offsets")
         x_tile = held.tile([P, BLOCKS * N], BF16, name="x_tile")
-        nc.scalar.dma_start(x_tile[:], x.rearrange("(p a) j -> p (a j)", a=BLOCKS))
+        w_halves = [held.tile([P, 2 * P], BF16, name=f"w_half{h}") for h in range(2)]
+        nc.scalar.dma_start(base_tile[:], base)
+        nc.sync.dma_start(offsets[:], offs)
+        nc.sync.dma_start(x_tile[:], x_rows)
+        nc.scalar.dma_start(w_halves[0][:], w_rows[:, 0 : 2 * P])
+        nc.sync.dma_start(w_halves[1][:], w_rows[:, 2 * P : 4 * P])
 
         identity = held.tile([P, P], BF16, name="identity")
         make_identity(nc, identity[:])
@@ -38,7 +40,7 @@ def tile_scatter_matmul_kernel(tc, base, x, w, offs, out):
         for a in range(BLOCKS):
             nc.tensor.matmul(
                 window[:].indirect(offsets[:]),
-                w_tile[:, a * P : (a + 1) * P],
+                w_halves[a // 2][:, (a % 2) * P : (a % 2 + 1) * P],
                 x_tile[:, a * N : (a + 1) * N],
                 start=False,
                 stop=(a == BLOCKS - 1),

@@ -25,11 +25,11 @@ def tile_scatter_matmul_kernel(tc, base, x, w, offs, out):
         offsets = held.tile([P, N // 16], U16, name="offsets")
         x_tile = held.tile([P, BLOCKS * N], BF16, name="x_tile")
         w_halves = [held.tile([P, 2 * P], BF16, name=f"w_half{h}") for h in range(2)]
-        nc.scalar.dma_start(base_tile[:], base)
         nc.sync.dma_start(offsets[:], offs)
-        nc.sync.dma_start(x_tile[:], x_rows)
+        nc.scalar.dma_start(base_tile[:], base)
+        nc.scalar.dma_start(x_tile[:], x_rows)
         nc.scalar.dma_start(w_halves[0][:], w_rows[:, 0 : 2 * P])
-        nc.sync.dma_start(w_halves[1][:], w_rows[:, 2 * P : 4 * P])
+        nc.scalar.dma_start(w_halves[1][:], w_rows[:, 2 * P : 4 * P])
 
         identity = held.tile([P, P], BF16, name="identity")
         make_identity(nc, identity[:])

@@ -25,11 +25,11 @@ def tile_scatter_matmul_kernel(tc, base, x, w, offs, out):
         offsets = held.tile([P, N // 16], U16, name="offsets")
         x_tile = held.tile([P, BLOCKS * N], BF16, name="x_tile")
         w_halves = [held.tile([P, 2 * P], BF16, name=f"w_half{h}") for h in range(2)]
+        nc.sync.dma_start(base_tile[:], base)
         nc.sync.dma_start(offsets[:], offs)
-        nc.scalar.dma_start(base_tile[:], base)
-        nc.scalar.dma_start(x_tile[:], x_rows)
-        nc.scalar.dma_start(w_halves[0][:], w_rows[:, 0 : 2 * P])
-        nc.scalar.dma_start(w_halves[1][:], w_rows[:, 2 * P : 4 * P])
+        nc.sync.dma_start(x_tile[:], x_rows)
+        nc.sync.dma_start(w_halves[0][:], w_rows[:, 0 : 2 * P])
+        nc.sync.dma_start(w_halves[1][:], w_rows[:, 2 * P : 4 * P])
 
         identity = held.tile([P, P], BF16, name="identity")
         make_identity(nc, identity[:])

@@ -9,6 +9,9 @@ N = 64
 K = 512
 BLOCKS = K // P
 
+WARM_COLUMNS = 512
+WARM_MATMULS = 3
+
 FLOPS = 2 * K * P * N
 
 
@@ -18,6 +21,18 @@ def tile_scatter_matmul_kernel(tc, base, x, w, offs, out):
         tc.tile_pool(name="held", bufs=1) as held,
         tc.psum_pool(name="psum", bufs=1) as psum,
     ):
+        zeros = held.tile([P, 2], BF16, name="zeros")
+        nc.vector.memset(zeros[:], 0.0)
+        unread = psum.tile([P, WARM_COLUMNS], F32, name="unread")
+        for _ in range(WARM_MATMULS):
+            nc.tensor.matmul(
+                unread[:],
+                zeros[:, 0:1].to_broadcast([P, P]),
+                zeros[:, 0:1].to_broadcast([P, WARM_COLUMNS]),
+                start=True,
+                stop=True,
+            )
+
         w_rows = w.rearrange("(p a) m -> p (a m)", a=BLOCKS)
         x_rows = x.rearrange("(p a) j -> p (a j)", a=BLOCKS)
 

@@ -12,6 +12,8 @@ BLOCKS = K // P
 WARM_COLUMNS = 512
 WARM_MATMULS = 3
 
+ROW_ALIGN = 256
+
 FLOPS = 2 * K * P * N
 
 
@@ -36,10 +38,12 @@ def tile_scatter_matmul_kernel(tc, base, x, w, offs, out):
         w_rows = w.rearrange("(p a) m -> p (a m)", a=BLOCKS)
         x_rows = x.rearrange("(p a) j -> p (a j)", a=BLOCKS)
 
-        base_tile = held.tile([P, S], BF16, name="base_tile")
+        base_tile = held.tile([P, S], BF16, name="base_tile", align_bytes=ROW_ALIGN)
         offsets = held.tile([P, N // 16], U16, name="offsets")
-        x_tile = held.tile([P, BLOCKS * N], BF16, name="x_tile")
-        w_halves = [held.tile([P, 2 * P], BF16, name=f"w_half{h}") for h in range(2)]
+        x_tile = held.tile([P, BLOCKS * N], BF16, name="x_tile", align_bytes=ROW_ALIGN)
+        w_halves = [
+            held.tile([P, 2 * P], BF16, name=f"w_half{h}", align_bytes=ROW_ALIGN) for h in range(2)
+        ]
         nc.sync.dma_start(base_tile[:], base)
         nc.sync.dma_start(offsets[:], offs)
         nc.sync.dma_start(x_tile[:], x_rows)
@@ -61,6 +65,6 @@ def tile_scatter_matmul_kernel(tc, base, x, w, offs, out):
                 stop=(a == BLOCKS - 1),
             )
 
-        z = held.tile([P, S], F32, name="z")
+        z = held.tile([P, S], F32, name="z", align_bytes=ROW_ALIGN)
         nc.vector.tensor_copy(z[:], window[:])
         nc.sync.dma_start(out, z[:])

@@ -10,7 +10,7 @@ K = 512
 BLOCKS = K // P
 
 WARM_COLUMNS = 512
-WARM_MATMULS = 3
+WARM_MATMULS = 2
 
 ROW_ALIGN = 256
 

@@ -23,7 +23,7 @@ def tile_scatter_matmul_kernel(tc, base, x, w, offs, out):
         tc.tile_pool(name="held", bufs=1) as held,
         tc.psum_pool(name="psum", bufs=1) as psum,
     ):
-        zeros = held.tile([P, 2], BF16, name="zeros")
+        zeros = held.tile([P, 1], BF16, name="zeros")
         nc.vector.memset(zeros[:], 0.0)
         unread = psum.tile([P, WARM_COLUMNS], F32, name="unread")
         for _ in range(WARM_MATMULS):

@@ -45,9 +45,9 @@ def tile_scatter_matmul_kernel(tc, base, x, w, offs, out):
             held.tile([P, 2 * P], BF16, name=f"w_half{h}", align_bytes=ROW_ALIGN) for h in range(2)
         ]
         nc.sync.dma_start(base_tile[:], base)
-        nc.sync.dma_start(offsets[:], offs)
         nc.sync.dma_start(x_tile[:], x_rows)
         nc.sync.dma_start(w_halves[0][:], w_rows[:, 0 : 2 * P])
+        nc.sync.dma_start(offsets[:], offs)
         nc.sync.dma_start(w_halves[1][:], w_rows[:, 2 * P : 4 * P])
 
         identity = held.tile([P, P], BF16, name="identity")

import concourse.mybir as mybir
from concourse.masks import make_identity

BF16, F32, U16 = mybir.dt.bfloat16, mybir.dt.float32, mybir.dt.uint16

P = 128
S = 256
N = 64
K = 512
BLOCKS = K // P

WARM_COLUMNS = 512
WARM_MATMULS = 2

ROW_ALIGN = 256

FLOPS = 2 * K * P * N


def tile_scatter_matmul_kernel(tc, base, x, w, offs, out):
    nc = tc.nc
    with (
        tc.tile_pool(name="held", bufs=1) as held,
        tc.psum_pool(name="psum", bufs=1) as psum,
    ):
        zeros = held.tile([P, 1], BF16, name="zeros")
        nc.vector.memset(zeros[:], 0.0)
        unread = psum.tile([P, WARM_COLUMNS], F32, name="unread")
        for _ in range(WARM_MATMULS):
            nc.tensor.matmul(
                unread[:],
                zeros[:, 0:1].to_broadcast([P, P]),
                zeros[:, 0:1].to_broadcast([P, WARM_COLUMNS]),
                start=True,
                stop=True,
            )

        w_rows = w.rearrange("(p a) m -> p (a m)", a=BLOCKS)
        x_rows = x.rearrange("(p a) j -> p (a j)", a=BLOCKS)

        base_tile = held.tile([P, S], BF16, name="base_tile", align_bytes=ROW_ALIGN)
        offsets = held.tile([P, N // 16], U16, name="offsets")
        x_tile = held.tile([P, BLOCKS * N], BF16, name="x_tile", align_bytes=ROW_ALIGN)
        w_halves = [
            held.tile([P, 2 * P], BF16, name=f"w_half{h}", align_bytes=ROW_ALIGN) for h in range(2)
        ]
        nc.sync.dma_start(base_tile[:], base)
        nc.sync.dma_start(x_tile[:], x_rows)
        nc.sync.dma_start(w_halves[0][:], w_rows[:, 0 : 2 * P])
        nc.sync.dma_start(offsets[:], offs)
        nc.sync.dma_start(w_halves[1][:], w_rows[:, 2 * P : 4 * P])

        identity = held.tile([P, P], BF16, name="identity")
        make_identity(nc, identity[:])

        window = psum.tile([P, S], F32, name="window")
        nc.tensor.matmul(window[:], identity[:], base_tile[:], start=True, stop=False)

        for a in range(BLOCKS):
            nc.tensor.matmul(
                window[:].indirect(offsets[:]),
                w_halves[a // 2][:, (a % 2) * P : (a % 2 + 1) * P],
                x_tile[:, a * N : (a + 1) * N],
                start=False,
                stop=(a == BLOCKS - 1),
            )

        z = held.tile([P, S], F32, name="z", align_bytes=ROW_ALIGN)
        nc.vector.tensor_copy(z[:], window[:])
        nc.sync.dma_start(out, z[:])
